import numpy as np, ml_dtypes
CORES = [32,40,48,56,64,72,80,88,96,104,112,120]
N = 12
T = 2048
def entries(a): return a.T.reshape(-1)
def pack(v, P): return np.ascontiguousarray(np.asarray(v, np.int32).reshape(-1, P).T)
def lists(rng, how):
    h = rng.integers(0, N * T, 8)
    if how == "zero": h[:] = 0
    if how == "blocks": h = T * rng.integers(1, N, 8)
    if how == "last": h[:] = N * T - 1
    if how == "mixed": h = T * rng.choice([q for q in range(N) if q & (q - 1)], 8) + rng.integers(1, T, 8)
    if how == "small": h = rng.permutation([0, 1, T - 1, T, T + 1, N * T - 1, T * int(rng.integers(2, N)), int(rng.integers(1, T))])
    return {"hh": np.broadcast_to(pack(np.concatenate([h, np.zeros(24, np.int64)]), 16), (N, 16, 2)).copy()}
def setup_inputs(rng):
    return dict({"x": rng.standard_normal((N, 128, T), dtype=np.float32).astype(ml_dtypes.bfloat16)}, **lists(rng, "uniform"))
def setup_inputs_blocks(rng):
    d = setup_inputs(rng); d.update(lists(rng, "blocks"))
    for k in ("x",): d[k] = (d[k].astype(np.float32) * 1048576.0).astype(d[k].dtype)
    return d
def setup_inputs_last(rng):
    d = setup_inputs(rng); d.update(lists(rng, "last"))
    for k in ("x",): d[k] = (d[k].astype(np.float32) * (1 / 1024.0)).astype(d[k].dtype)
    return d
def setup_inputs_mixed(rng):
    d = setup_inputs(rng); d.update(lists(rng, "mixed"))
    return d
def setup_inputs_small(rng):
    d = setup_inputs(rng); d.update(lists(rng, "small"))
    return d
def setup_inputs_zero(rng):
    d = setup_inputs(rng); d.update(lists(rng, "zero"))
    return d
def check_inputs(x):
    bad = []
    if x["hh"].min() < 0 or x["hh"].max() >= N * T: bad.append("hh out of range")
    if entries(x["hh"][0])[8:].any(): bad.append("an entry that should be 0 isn't")
    if not all(np.array_equal(a, x["hh"][0]) for a in x["hh"]): bad.append("hh isn't alike on all ranks")
    return bad
def reference(x, hh):
    h = entries(hh[0]); A = np.concatenate(list(x), axis=1)
    Y = np.concatenate([np.roll(A[16 * k:16 * k + 16], -int(h[k]), axis=1) for k in range(8)], axis=0)
    return {"y": np.stack([Y[:, T * r:T * r + T] for r in range(N)])}

@@ -1,0 +1,265 @@
+from concourse.bass import DstId, RemoteDMATransfer
+from concourse.mybir import AluOpType, ActivationFunctionType
+
+N = 12
+COLS = 2048
+W = 176
+STEP = 170
+HALF = 1022
+HW = 1026
+PAIR = STEP + W
+NW = N * W
+K = W // 16
+ZW = NW + 8
+LC = N * K
+
+SCRATCH = {
+    "XC": ("sbuf", [128, HW], "bfloat16"), "XS": ("sbuf", [128, HW], "bfloat16"),
+    "W": ("sbuf", [128, NW], "bfloat16"),
+    "OUT": ("sbuf", [128, NW], "bfloat16"),
+    "Z": ("sbuf", [128, ZW], "bfloat16"),
+    "YO": ("sbuf", [128, COLS], "bfloat16"),
+    "HA": ("sbuf", [128, PAIR], "bfloat16"), "HB": ("sbuf", [128, 2 * W], "bfloat16"),
+    "HH": ("sbuf", [128, 2], "int32"), "HF": ("sbuf", [128, 1], "float32"),
+    "SI": ("sbuf", [128, 128], "int32"), "SJ": ("sbuf", [128, 128], "int32"), "SEL": ("sbuf", [128, 128], "float32"),
+    "PI": ("sbuf", [128, 1], "int32"), "PJ": ("sbuf", [128, 1], "int32"),
+    "PM": ("sbuf", [128, 1], "float32"), "NPM": ("sbuf", [128, 1], "float32"),
+    "HI": ("sbuf", [128, 1], "int32"), "QI": ("sbuf", [128, 1], "int32"), "RI": ("sbuf", [128, 1], "int32"),
+    "SP": ("sbuf", [128, 1], "float32"), "SM": ("sbuf", [128, 1], "float32"),
+    "QW": ("sbuf", [128, 1], "float32"), "THR": ("sbuf", [128, 1], "float32"),
+    "TA": ("sbuf", [128, LC], "int32"), "E": ("sbuf", [128, LC], "int32"),
+    "M": ("sbuf", [128, LC], "int32"), "V": ("sbuf", [128, LC], "int32"),
+    "O": ("sbuf", [128, LC], "int32"), "R": ("sbuf", [128, LC], "int32"), "L1": ("sbuf", [128, LC + 4], "uint16"),
+    "I0": ("sbuf", [128, 128], "int32"), "A": ("sbuf", [128, 128], "int32"), "RHO": ("sbuf", [128, 128], "int32"),
+    "B3": ("sbuf", [128, 128], "int32"), "BJ": ("sbuf", [128, 128], "int32"), "H6": ("sbuf", [128, 128], "int32"),
+    "E6": ("sbuf", [128, 128], "int32"), "F": ("sbuf", [128, 128], "int32"), "F2": ("sbuf", [128, 128], "int32"),
+    "L2": ("sbuf", [128, 128], "uint16"),
+    "ps": ("psum", [128, 8], "float32"),
+}
+SEMAPHORES = ["ldc", "lds", "ldo", "ldh", "io1", "io2", "io3", "vc", "pe", "arr1", "arr2", "ha", "hb",
+              "loc", "gv1", "gv2", "gs1", "gs2", "y0", "y1", "y2", "y3", "st", "st2"]
+
+
+def engines(mask):
+    return [e for e in range(mask.bit_length()) if (mask >> e) & 1]
+
+
+def bitmask(es):
+    return sum(1 << e for e in es)
+
+
+def planes(T, topo):
+    c0 = topo.chip(T.cores[0])
+    a = [r for r in range(N) if r == 0 or topo.same_plane(c0, topo.chip(T.cores[r]))]
+    return [a, [r for r in range(N) if r not in a]]
+
+
+def place(r, pl):
+    half = 0 if r in pl[0] else 1
+    return half, pl[half].index(r)
+
+
+def start(r, pl):
+    half, b = place(r, pl)
+    return HALF * half + STEP * b
+
+
+def zslot(r, pl):
+    half, b = place(r, pl)
+    return W * (6 * half + b) + 8 * half
+
+
+def carriers(rank, T, topo, pl):
+    core = T.cores[rank]
+    far = T.cores[pl[1 - place(rank, pl)[0]][0]]
+    own = [c for c in range(topo.CHIPS * topo.CORES_PER_CHIP)
+           if c != core and topo.chip(c) == topo.chip(core) and topo.may_write(c, far)]
+    return ([c for c in own if topo.die(c) != topo.die(core)] + [c for c in own if topo.die(c) == topo.die(core)])[:3]
+
+
+def dst(core, topo):
+    rid, pid, _ = topo.addr(core)
+    return DstId(rid=rid, pnc=pid)
+
+
+def send(mask_engines, src, out, to, sem, topo):
+    return RemoteDMATransfer(dst_ids=[dst(to, topo)], dma_engine_mask=bitmask(mask_engines), remote_sem=sem,
+                             src=src, dst=out)
+
+
+def carrier_program(g, core, rank, u, T, topo, pl):
+    half, a = place(rank, pl)
+    v = (u - a) % 3
+    to = [pl[1 - half][2 * v], pl[1 - half][2 * v + 1]]
+    n = 0
+    zs = zslot(rank, pl)
+    es = engines(topo.mask(core, T.cores[to[0]]))
+    h = len(es) // 2
+    for sem, buf, step, out, arr in ((T.sem.ha, T.HA, STEP, T.W[:, rank * W:(rank + 1) * W], T.sem.arr1),
+                                     (T.sem.hb, T.HB, W, T.Z[:, zs:zs + W], T.sem.arr2)):
+        g.wait_ge(sem, 4)
+        g.remote_dma_fused([send(es[i * h:(i + 1) * h], buf[:, i * step:i * step + W], out, T.cores[to[i]], arr, topo)
+                            for i in range(2)], local_sem=T.sem.loc)
+        n += 2 * h
+    g.wait_ge(T.sem.loc, n)
+
+
+def rank_program(g, core, T, topo):
+    pl = planes(T, topo)
+    rank = T.rank_of(core)
+    if rank is None:
+        for r in range(N):
+            if topo.chip(T.cores[r]) == topo.chip(core):
+                cs = carriers(r, T, topo, pl)
+                if core in cs:
+                    carrier_program(g, core, r, cs.index(core), T, topo, pl)
+        return
+    half, a = place(rank, pl)
+    cross = pl[1 - half]
+    others = [pl[half][(a + k) % 6] for k in range(1, 6)]
+    cs = carriers(rank, T, topo, pl)
+    off = engines(topo.mask(core, T.cores[others[0]]))
+    on = engines(topo.mask(core, cs[0]))
+    order = [e for e in on if e not in off] + off[::-1]
+    hop = [order[4 * u:4 * u + 4] for u in range(3)]
+    add, mult, lt, ge, eq = AluOpType.add, AluOpType.mult, AluOpType.is_lt, AluOpType.is_ge, AluOpType.is_equal
+    shr, band = AluOpType.arith_shift_right, AluOpType.bitwise_and
+    copy = ActivationFunctionType.Copy
+
+    lo_c, lo_s = HALF * (1 - half), HALF * half
+    g.sync.dma_start(T.XC[:, :], T.x[:, lo_c:lo_c + HW]).then_inc(T.sem.ldc, 16)
+    g.sync.dma_start(T.XS[:, :], T.x[:, lo_s:lo_s + HW]).then_inc(T.sem.lds, 16)
+    g.scalar.dma_start(T.HH[0:16, 0:2], T.hh[:, :]).then_inc(T.sem.ldh, 16)
+    s0 = start(rank, pl)
+    g.scalar.dma_start(T.W[:, rank * W:(rank + 1) * W], T.x[:, s0:s0 + W]).then_inc(T.sem.ldo, 16)
+
+    g.iota(T.SI[0:16, :], [[1, 128]], 0, -16).then_inc(T.sem.io1, 1)
+    g.iota(T.PI[:, 0:1], [[1, 1]], 0, 1).then_inc(T.sem.io1, 1)
+    g.iota(T.TA[:, :], [[0, 12], [16, K]], s0, 1).then_inc(T.sem.io2, 1)
+    n2 = 1
+    for lst, c in ((cross, 0), (others + [rank], 6 * K)):
+        i = 0
+        while i < len(lst):
+            j = i + 1
+            while j < len(lst) and lst[j] - lst[j - 1] == lst[i + 1] - lst[i]:
+                j += 1
+            step = lst[i + 1] - lst[i] if j > i + 1 else 0
+            g.iota(T.E[:, c + i * K:c + j * K], [[step * W, j - i], [16, K]], lst[i] * W, 1).then_inc(T.sem.io2, 1)
+            n2 += 1
+            i = j
+
+    nloc = 0
+    g.wait_ge(T.sem.ldc, 16)
+    g.remote_dma_fused([send(hop[u], T.XC[:, 2 * STEP * ((u - a) % 3):2 * STEP * ((u - a) % 3) + PAIR], T.HA[:, :], cs[u],
+                             T.sem.ha, topo) for u in range(3)], local_sem=T.sem.loc)
+    nloc += 12
+    g.wait_ge(T.sem.lds, 16)
+
+    def piece(k):
+        b = place(others[k], pl)[1]
+        return T.XS[:, STEP * b:STEP * b + W]
+
+    def direct(src, out, arr):
+        g.remote_dma_fused([send(off[2 * k:2 * k + 2], src(k), out, T.cores[others[k]], arr, topo) for k in range(4)],
+                           local_sem=T.sem.loc)
+        rid, pid, _ = topo.addr(T.cores[others[4]])
+        g.remote_dma(out, src(4), arr, T.sem.loc, pid, rid, bitmask(off))
+        return 8 + len(off)
+    nloc += direct(piece, T.W[:, rank * W:(rank + 1) * W], T.sem.arr1)
+    g.iota(T.I0[:, :], [[16, 128]], 0, 1).then_inc(T.sem.io3, 1)
+
+    vec = g.vector
+    n = [0]
+
+    def v(ins):
+        ins.then_inc(T.sem.vc, 1)
+        n[0] += 1
+        vec.wait_ge(T.sem.vc, n[0])
+    vec.wait_ge(T.sem.io1, 2)
+    v(vec.tensor_scalar(T.SJ[0:16, :], T.SI[0:16, :], 4, None, shr))
+    v(vec.tensor_scalar(T.SEL[0:16, :], T.SJ[0:16, :], 0, None, eq))
+    v(vec.tensor_scalar(T.PJ[:, 0:1], T.PI[:, 0:1], 4, None, shr))
+    v(vec.tensor_scalar(T.PM[:, 0:1], T.PJ[:, 0:1], 16, None, mult))
+    v(vec.tensor_scalar(T.NPM[:, 0:1], T.PJ[:, 0:1], -16, None, mult))
+    vec.wait_ge(T.sem.ldh, 16)
+    v(vec.tensor_copy(T.HF[0:16, 0:1], T.HH[0:16, 0:1]))
+    g.tensor.wait_ge(T.sem.vc, n[0])
+    g.tensor.matmul(T.ps[:, 0:1], T.SEL[0:16, :], T.HF[0:16, 0:1], True, True).then_inc(T.sem.pe, 1)
+    vec.wait_ge(T.sem.pe, 1)
+    v(vec.tensor_copy(T.HI[:, 0:1], T.ps[:, 0:1]))
+    v(vec.tensor_scalar(T.QI[:, 0:1], T.HI[:, 0:1], 11, None, shr))
+    v(vec.tensor_scalar(T.RI[:, 0:1], T.HI[:, 0:1], COLS - 1, None, band))
+    v(vec.tensor_scalar(T.SP[:, 0:1], T.RI[:, 0:1], T.PM[:, 0:1], None, add))
+    v(vec.tensor_scalar(T.SM[:, 0:1], T.RI[:, 0:1], T.NPM[:, 0:1], None, add))
+    v(vec.tensor_scalar(T.QW[:, 0:1], T.QI[:, 0:1], W, T.NPM[:, 0:1], mult, add))
+    v(vec.tensor_scalar(T.THR[:, 0:1], T.QW[:, 0:1], -1, NW, mult, add))
+    vec.wait_ge(T.sem.io2, n2)
+    v(vec.tensor_scalar(T.M[:, :], T.TA[:, :], T.SP[:, 0:1], W, lt, mult))
+    v(vec.tensor_tensor(T.V[:, :], T.E[:, :], T.M[:, :], add))
+    v(vec.tensor_scalar(T.O[:, :], T.V[:, :], T.THR[:, 0:1], -NW, ge, mult))
+    v(vec.tensor_tensor(T.R[:, :], T.V[:, :], T.O[:, :], add))
+    at = {0: 0, 3: 3 * K + 1, 6: 6 * K + 2, 8: 8 * K + 2, 11: 11 * K + 3}
+    for lo, hi in ((0, 3), (3, 6), (6, 11), (11, 12)):
+        vec.tensor_scalar(T.L1[:, at[lo]:at[lo] + (hi - lo) * K], T.R[:, lo * K:hi * K], T.QW[:, 0:1], None,
+                          add).then_inc(T.sem.vc, 1)
+        n[0] += 1
+    vec.wait_ge(T.sem.vc, n[0])
+
+    g.scalar.wait_ge(T.sem.vc, n[0])
+    for q in (vec, g.scalar):
+        q.wait_ge(T.sem.ldo, 16)
+        q.wait_ge(T.sem.arr1, 40)
+
+    def pick(lo, hi):
+        return T.W[:, :].indirect(T.L1[:, at[lo]:at[lo] + (hi - lo) * K])
+    zs = zslot(rank, pl)
+    vec.tensor_copy(T.OUT[:, 0:3 * W], pick(0, 3)).then_inc(T.sem.gv1, 1)
+    vec.tensor_copy(T.OUT[:, 6 * W:8 * W], pick(6, 8)).then_inc(T.sem.gv2, 1)
+    vec.tensor_copy(T.Z[:, zs:zs + W], pick(11, 12)).then_inc(T.sem.gv2, 1)
+    g.scalar.activation(T.OUT[:, 3 * W:6 * W], pick(3, 6), copy).then_inc(T.sem.gs1, 1)
+    g.scalar.activation(T.OUT[:, 8 * W:11 * W], pick(8, 11), copy).then_inc(T.sem.gs2, 1)
+
+    g.wait_ge(T.sem.gv1, 1)
+    g.wait_ge(T.sem.gs1, 1)
+    g.remote_dma_fused([send(hop[u], T.OUT[:, 2 * W * ((u - a) % 3):2 * W * ((u - a) % 3) + 2 * W], T.HB[:, :], cs[u],
+                             T.sem.hb, topo) for u in range(3)], local_sem=T.sem.loc)
+    nloc += 12
+    g.wait_ge(T.sem.gv2, 2)
+    g.wait_ge(T.sem.gs2, 1)
+    nloc += direct(lambda k: T.OUT[:, (6 + k) * W:(7 + k) * W], T.Z[:, zs:zs + W], T.sem.arr2)
+
+    vec.wait_ge(T.sem.io3, 1)
+    v(vec.tensor_scalar(T.A[:, :], T.I0[:, :], T.SM[:, 0:1], None, add))
+    v(vec.tensor_scalar(T.RHO[:, :], T.A[:, :], COLS - 1, None, band))
+    v(vec.tensor_scalar(T.B3[:, :], T.RHO[:, :], 3, None, mult))
+    v(vec.tensor_scalar(T.BJ[:, :], T.B3[:, :], 9, None, shr))
+    v(vec.tensor_scalar(T.E6[:, :], T.BJ[:, :], 6, None, mult))
+    v(vec.tensor_scalar(T.H6[:, :], T.RHO[:, :], 1024, 6, ge, mult))
+    v(vec.tensor_tensor(T.F[:, :], T.E6[:, :], T.RHO[:, :], add))
+    v(vec.tensor_tensor(T.F2[:, :], T.F[:, :], T.H6[:, :], add))
+    v(vec.tensor_copy(T.L2[:, :], T.F2[:, :]))
+
+    g.scalar.wait_ge(T.sem.vc, n[0])
+    g.scalar.wait_ge(T.sem.gv2, 2)
+    vec.wait_ge(T.sem.gv2, 2)
+    for q in (vec, g.scalar):
+        q.wait_ge(T.sem.arr2, 40)
+
+    def turn(b):
+        return T.YO[:, 512 * b:512 * b + 512], T.Z[:, :].indirect(T.L2[:, 32 * b:32 * b + 32])
+    out, src = turn(0)
+    vec.tensor_copy(out, src).then_inc(T.sem.y0, 1)
+    out, src = turn(1)
+    vec.tensor_copy(out, src).then_inc(T.sem.y1, 1)
+    out, src = turn(2)
+    g.scalar.activation(out, src, copy).then_inc(T.sem.y2, 1)
+    out, src = turn(3)
+    g.scalar.activation(out, src, copy).then_inc(T.sem.y3, 1)
+    for b, sem in ((0, T.sem.y0), (2, T.sem.y2), (1, T.sem.y1)):
+        g.sync.wait_ge(sem, 1)
+        g.sync.dma_start(T.y[:, 512 * b:512 * b + 512], T.YO[:, 512 * b:512 * b + 512]).then_inc(T.sem.st, 16)
+    g.scalar.wait_ge(T.sem.y3, 1)
+    g.scalar.dma_start(T.y[:, 1536:2048], T.YO[:, 1536:2048]).then_inc(T.sem.st2, 16)
+    g.sync.wait_ge(T.sem.st, 48)
+    g.scalar.wait_ge(T.sem.st2, 16)
+    g.wait_ge(T.sem.loc, nloc)

@@ -3,23 +3,21 @@ from concourse.mybir import AluOpType, ActivationFunctionType
 
 N = 12
 COLS = 2048
-W = 176
-STEP = 170
+W = 171
+G = 176
 HALF = 1022
-HW = 1026
-PAIR = STEP + W
+HW = 6 * W
 NW = N * W
-K = W // 16
-ZW = NW + 8
+K = G // 16
 LC = N * K
 
 SCRATCH = {
     "XC": ("sbuf", [128, HW], "bfloat16"), "XS": ("sbuf", [128, HW], "bfloat16"),
     "W": ("sbuf", [128, NW], "bfloat16"),
-    "OUT": ("sbuf", [128, NW], "bfloat16"),
-    "Z": ("sbuf", [128, ZW], "bfloat16"),
+    "OUT": ("sbuf", [128, N * G], "bfloat16"),
+    "Z": ("sbuf", [128, NW], "bfloat16"),
     "YO": ("sbuf", [128, COLS], "bfloat16"),
-    "HA": ("sbuf", [128, PAIR], "bfloat16"), "HB": ("sbuf", [128, 2 * W], "bfloat16"),
+    "HA": ("sbuf", [128, 2 * W], "bfloat16"), "HB": ("sbuf", [128, G + W], "bfloat16"),
     "HH": ("sbuf", [128, 2], "int32"), "HF": ("sbuf", [128, 1], "float32"),
     "SI": ("sbuf", [128, 128], "int32"), "SJ": ("sbuf", [128, 128], "int32"), "SEL": ("sbuf", [128, 128], "float32"),
     "PI": ("sbuf", [128, 1], "int32"), "PJ": ("sbuf", [128, 1], "int32"),
@@ -29,15 +27,13 @@ SCRATCH = {
     "QW": ("sbuf", [128, 1], "float32"), "THR": ("sbuf", [128, 1], "float32"),
     "TA": ("sbuf", [128, LC], "int32"), "E": ("sbuf", [128, LC], "int32"),
     "M": ("sbuf", [128, LC], "int32"), "V": ("sbuf", [128, LC], "int32"),
-    "O": ("sbuf", [128, LC], "int32"), "R": ("sbuf", [128, LC], "int32"), "L1": ("sbuf", [128, LC + 4], "uint16"),
+    "O": ("sbuf", [128, LC], "int32"), "R": ("sbuf", [128, LC], "int32"), "L1": ("sbuf", [128, LC + 8], "uint16"),
     "I0": ("sbuf", [128, 128], "int32"), "A": ("sbuf", [128, 128], "int32"), "RHO": ("sbuf", [128, 128], "int32"),
-    "B3": ("sbuf", [128, 128], "int32"), "BJ": ("sbuf", [128, 128], "int32"), "H6": ("sbuf", [128, 128], "int32"),
-    "E6": ("sbuf", [128, 128], "int32"), "F": ("sbuf", [128, 128], "int32"), "F2": ("sbuf", [128, 128], "int32"),
-    "L2": ("sbuf", [128, 128], "uint16"),
+    "H4": ("sbuf", [128, 128], "int32"), "F": ("sbuf", [128, 128], "int32"), "L2": ("sbuf", [128, 128], "uint16"),
     "ps": ("psum", [128, 8], "float32"),
 }
-SEMAPHORES = ["ldc", "lds", "ldo", "ldh", "io1", "io2", "io3", "vc", "pe", "arr1", "arr2", "ha", "hb",
-              "loc", "gv1", "gv2", "gs1", "gs2", "y0", "y1", "y2", "y3", "st", "st2"]
+SEMAPHORES = ["ldc", "lds", "own1", "own2", "ldh", "io1", "tab", "vc", "pe", "arr1", "arr2", "ha", "hb",
+              "loc", "gv1", "gv2", "gv3", "gs1", "gs2", "gs3", "y0", "y1", "y2", "y3", "st", "st2"]
 
 
 def engines(mask):
@@ -61,46 +57,72 @@ def place(r, pl):
 
 def start(r, pl):
     half, b = place(r, pl)
-    return HALF * half + STEP * b
+    return HALF * half + W * b
 
 
 def zslot(r, pl):
     half, b = place(r, pl)
-    return W * (6 * half + b) + 8 * half
+    return HW * half + W * b
+
+
+def destinations(rank, pl):
+    half, a = place(rank, pl)
+    return pl[1 - half], [pl[half][(a + k) % 6] for k in range(1, 6)] + [rank]
 
 
 def carriers(rank, T, topo, pl):
     core = T.cores[rank]
     far = T.cores[pl[1 - place(rank, pl)[0]][0]]
-    own = [c for c in range(topo.CHIPS * topo.CORES_PER_CHIP)
-           if c != core and topo.chip(c) == topo.chip(core) and topo.may_write(c, far)]
-    return ([c for c in own if topo.die(c) != topo.die(core)] + [c for c in own if topo.die(c) == topo.die(core)])[:3]
-
-
-def dst(core, topo):
-    rid, pid, _ = topo.addr(core)
-    return DstId(rid=rid, pnc=pid)
+    chip = [c for c in range(topo.CHIPS * topo.CORES_PER_CHIP) if c != core and topo.chip(c) == topo.chip(core)]
+    chip = [c for c in chip if topo.die(c) != topo.die(core)] + [c for c in chip if topo.die(c) == topo.die(core)]
+    port = [c for c in chip if topo.may_write(c, far)][:3]
+    return port + [c for c in chip if c not in port][:1]
 
 
 def send(mask_engines, src, out, to, sem, topo):
-    return RemoteDMATransfer(dst_ids=[dst(to, topo)], dma_engine_mask=bitmask(mask_engines), remote_sem=sem,
+    rid, pid, _ = topo.addr(to)
+    return RemoteDMATransfer(dst_ids=[DstId(rid=rid, pnc=pid)], dma_engine_mask=bitmask(mask_engines), remote_sem=sem,
                              src=src, dst=out)
+
+
+def table(g, rank, u, T, pl):
+    if u == 0:
+        g.iota(T.TA[:, :], [[0, N], [16, K]], start(rank, pl), 1).then_inc(T.sem.io1, 1)
+        return T.TA[:, :], 1
+    if u == 3:
+        g.iota(T.I0[:, :], [[16, 128]], 0, 1).then_inc(T.sem.io1, 1)
+        return T.I0[:, :], 1
+    n = i = 0
+    lst, c = destinations(rank, pl)[u - 1], 6 * K * (u - 1)
+    while i < len(lst):
+        j = i + 1
+        while j < len(lst) and lst[j] - lst[j - 1] == lst[i + 1] - lst[i]:
+            j += 1
+        step = lst[i + 1] - lst[i] if j > i + 1 else 0
+        g.iota(T.E[:, c + i * K:c + j * K], [[step * W, j - i], [16, K]], lst[i] * W, 1).then_inc(T.sem.io1, 1)
+        n += 1
+        i = j
+    return T.E[:, c:c + 6 * K], n
 
 
 def carrier_program(g, core, rank, u, T, topo, pl):
     half, a = place(rank, pl)
     v = (u - a) % 3
-    to = [pl[1 - half][2 * v], pl[1 - half][2 * v + 1]]
-    n = 0
+    to = [pl[1 - half][2 * v], pl[1 - half][2 * v + 1]] if u < 3 else [destinations(rank, pl)[1][4]]
     zs = zslot(rank, pl)
     es = engines(topo.mask(core, T.cores[to[0]]))
-    h = len(es) // 2
-    for sem, buf, step, out, arr in ((T.sem.ha, T.HA, STEP, T.W[:, rank * W:(rank + 1) * W], T.sem.arr1),
-                                     (T.sem.hb, T.HB, W, T.Z[:, zs:zs + W], T.sem.arr2)):
-        g.wait_ge(sem, 4)
+    h = len(es) // len(to)
+    buf, n = table(g, rank, u, T, pl)
+    g.wait_ge(T.sem.io1, n)
+    rid, pid, _ = topo.addr(T.cores[rank])
+    g.remote_dma(buf, buf, T.sem.tab, T.sem.loc, pid, rid, bitmask(es))
+    n = len(es)
+    for sem, buf, step, out, arr in ((T.sem.ha, T.HA, W, T.W[:, rank * W:(rank + 1) * W], T.sem.arr1),
+                                     (T.sem.hb, T.HB, G, T.Z[:, zs:zs + W], T.sem.arr2)):
+        g.wait_ge(sem, 4 if u < 3 else 8)
         g.remote_dma_fused([send(es[i * h:(i + 1) * h], buf[:, i * step:i * step + W], out, T.cores[to[i]], arr, topo)
-                            for i in range(2)], local_sem=T.sem.loc)
-        n += 2 * h
+                            for i in range(len(to))], local_sem=T.sem.loc)
+        n += len(es)
     g.wait_ge(T.sem.loc, n)
 
 
@@ -115,58 +137,50 @@ def rank_program(g, core, T, topo):
                     carrier_program(g, core, r, cs.index(core), T, topo, pl)
         return
     half, a = place(rank, pl)
-    cross = pl[1 - half]
-    others = [pl[half][(a + k) % 6] for k in range(1, 6)]
+    others = destinations(rank, pl)[1][:5]
     cs = carriers(rank, T, topo, pl)
     off = engines(topo.mask(core, T.cores[others[0]]))
     on = engines(topo.mask(core, cs[0]))
     order = [e for e in on if e not in off] + off[::-1]
     hop = [order[4 * u:4 * u + 4] for u in range(3)]
     add, mult, lt, ge, eq = AluOpType.add, AluOpType.mult, AluOpType.is_lt, AluOpType.is_ge, AluOpType.is_equal
-    shr, band = AluOpType.arith_shift_right, AluOpType.bitwise_and
+    shr, band, low = AluOpType.arith_shift_right, AluOpType.bitwise_and, AluOpType.min
     copy = ActivationFunctionType.Copy
+    zs, s0 = zslot(rank, pl), start(rank, pl)
 
     lo_c, lo_s = HALF * (1 - half), HALF * half
     g.sync.dma_start(T.XC[:, :], T.x[:, lo_c:lo_c + HW]).then_inc(T.sem.ldc, 16)
     g.sync.dma_start(T.XS[:, :], T.x[:, lo_s:lo_s + HW]).then_inc(T.sem.lds, 16)
+    g.sync.dma_start(T.W[:, rank * W:(rank + 1) * W], T.x[:, s0:s0 + W]).then_inc(T.sem.own1, 16)
     g.scalar.dma_start(T.HH[0:16, 0:2], T.hh[:, :]).then_inc(T.sem.ldh, 16)
-    s0 = start(rank, pl)
-    g.scalar.dma_start(T.W[:, rank * W:(rank + 1) * W], T.x[:, s0:s0 + W]).then_inc(T.sem.ldo, 16)
-
     g.iota(T.SI[0:16, :], [[1, 128]], 0, -16).then_inc(T.sem.io1, 1)
     g.iota(T.PI[:, 0:1], [[1, 1]], 0, 1).then_inc(T.sem.io1, 1)
-    g.iota(T.TA[:, :], [[0, 12], [16, K]], s0, 1).then_inc(T.sem.io2, 1)
-    n2 = 1
-    for lst, c in ((cross, 0), (others + [rank], 6 * K)):
-        i = 0
-        while i < len(lst):
-            j = i + 1
-            while j < len(lst) and lst[j] - lst[j - 1] == lst[i + 1] - lst[i]:
-                j += 1
-            step = lst[i + 1] - lst[i] if j > i + 1 else 0
-            g.iota(T.E[:, c + i * K:c + j * K], [[step * W, j - i], [16, K]], lst[i] * W, 1).then_inc(T.sem.io2, 1)
-            n2 += 1
-            i = j
 
     nloc = 0
-    g.wait_ge(T.sem.ldc, 16)
-    g.remote_dma_fused([send(hop[u], T.XC[:, 2 * STEP * ((u - a) % 3):2 * STEP * ((u - a) % 3) + PAIR], T.HA[:, :], cs[u],
-                             T.sem.ha, topo) for u in range(3)], local_sem=T.sem.loc)
-    nloc += 12
-    g.wait_ge(T.sem.lds, 16)
+
+    def to_ports(src, step, out, sem):
+        g.remote_dma_fused([send(hop[u], src[:, 2 * step * ((u - a) % 3):2 * step * ((u - a) % 3) + step + W], out[:, :],
+                                 cs[u], sem, topo) for u in range(3)], local_sem=T.sem.loc)
+        return 12
+
+    def straight(src, out, arr):
+        g.remote_dma_fused([send(off[2 * k:2 * k + 2], src(k), out, T.cores[others[k]], arr, topo) for k in range(4)],
+                           local_sem=T.sem.loc)
+        return 8
+
+    def to_die(src, out, sem):
+        rid, pid, _ = topo.addr(cs[3])
+        g.remote_dma(out[:, 0:W], src(4), sem, T.sem.loc, pid, rid, bitmask(order[:8]))
+        return 8
 
     def piece(k):
         b = place(others[k], pl)[1]
-        return T.XS[:, STEP * b:STEP * b + W]
-
-    def direct(src, out, arr):
-        g.remote_dma_fused([send(off[2 * k:2 * k + 2], src(k), out, T.cores[others[k]], arr, topo) for k in range(4)],
-                           local_sem=T.sem.loc)
-        rid, pid, _ = topo.addr(T.cores[others[4]])
-        g.remote_dma(out, src(4), arr, T.sem.loc, pid, rid, bitmask(off))
-        return 8 + len(off)
-    nloc += direct(piece, T.W[:, rank * W:(rank + 1) * W], T.sem.arr1)
-    g.iota(T.I0[:, :], [[16, 128]], 0, 1).then_inc(T.sem.io3, 1)
+        return T.XS[:, W * b:W * b + W]
+    g.wait_ge(T.sem.ldc, 16)
+    nloc += to_ports(T.XC, W, T.HA, T.sem.ha)
+    g.wait_ge(T.sem.lds, 16)
+    nloc += straight(piece, T.W[:, rank * W:(rank + 1) * W], T.sem.arr1)
+    nloc += to_die(piece, T.HA, T.sem.ha)
 
     vec = g.vector
     n = [0]
@@ -193,56 +207,57 @@ def rank_program(g, core, T, topo):
     v(vec.tensor_scalar(T.SM[:, 0:1], T.RI[:, 0:1], T.NPM[:, 0:1], None, add))
     v(vec.tensor_scalar(T.QW[:, 0:1], T.QI[:, 0:1], W, T.NPM[:, 0:1], mult, add))
     v(vec.tensor_scalar(T.THR[:, 0:1], T.QW[:, 0:1], -1, NW, mult, add))
-    vec.wait_ge(T.sem.io2, n2)
+    vec.wait_ge(T.sem.tab, 4 * len(off))
     v(vec.tensor_scalar(T.M[:, :], T.TA[:, :], T.SP[:, 0:1], W, lt, mult))
     v(vec.tensor_tensor(T.V[:, :], T.E[:, :], T.M[:, :], add))
     v(vec.tensor_scalar(T.O[:, :], T.V[:, :], T.THR[:, 0:1], -NW, ge, mult))
     v(vec.tensor_tensor(T.R[:, :], T.V[:, :], T.O[:, :], add))
-    at = {0: 0, 3: 3 * K + 1, 6: 6 * K + 2, 8: 8 * K + 2, 11: 11 * K + 3}
+    at = {}
+    c = 0
     for lo, hi in ((0, 3), (3, 6), (6, 11), (11, 12)):
-        vec.tensor_scalar(T.L1[:, at[lo]:at[lo] + (hi - lo) * K], T.R[:, lo * K:hi * K], T.QW[:, 0:1], None,
-                          add).then_inc(T.sem.vc, 1)
+        vec.tensor_scalar(T.L1[:, c:c + (hi - lo) * K], T.R[:, lo * K:hi * K], T.QW[:, 0:1], NW - 1, add,
+                          low).then_inc(T.sem.vc, 1)
+        for i in range(lo, hi):
+            at[i] = c + (i - lo) * K
+        c += (hi - lo) * K
+        c += c % 2
         n[0] += 1
     vec.wait_ge(T.sem.vc, n[0])
 
     g.scalar.wait_ge(T.sem.vc, n[0])
     for q in (vec, g.scalar):
-        q.wait_ge(T.sem.ldo, 16)
+        q.wait_ge(T.sem.own1, 16)
         q.wait_ge(T.sem.arr1, 40)
 
     def pick(lo, hi):
         return T.W[:, :].indirect(T.L1[:, at[lo]:at[lo] + (hi - lo) * K])
-    zs = zslot(rank, pl)
-    vec.tensor_copy(T.OUT[:, 0:3 * W], pick(0, 3)).then_inc(T.sem.gv1, 1)
-    vec.tensor_copy(T.OUT[:, 6 * W:8 * W], pick(6, 8)).then_inc(T.sem.gv2, 1)
-    vec.tensor_copy(T.Z[:, zs:zs + W], pick(11, 12)).then_inc(T.sem.gv2, 1)
-    g.scalar.activation(T.OUT[:, 3 * W:6 * W], pick(3, 6), copy).then_inc(T.sem.gs1, 1)
-    g.scalar.activation(T.OUT[:, 8 * W:11 * W], pick(8, 11), copy).then_inc(T.sem.gs2, 1)
+    for lo, hi, sem in ((0, 3, T.sem.gv1), (6, 8, T.sem.gv2), (11, 12, T.sem.gv3)):
+        vec.tensor_copy(T.OUT[:, lo * G:hi * G], pick(lo, hi)).then_inc(sem, 1)
+    for lo, hi, sem in ((3, 6, T.sem.gs1), (8, 10, T.sem.gs2), (10, 11, T.sem.gs3)):
+        g.scalar.activation(T.OUT[:, lo * G:hi * G], pick(lo, hi), copy).then_inc(sem, 1)
+    g.sync.wait_ge(T.sem.gv3, 1)
+    g.sync.dma_start(T.Z[:, zs:zs + W], T.OUT[:, 11 * G:11 * G + W]).then_inc(T.sem.own2, 16)
 
+    def gathered(k):
+        return T.OUT[:, (6 + k) * G:(6 + k) * G + W]
     g.wait_ge(T.sem.gv1, 1)
     g.wait_ge(T.sem.gs1, 1)
-    g.remote_dma_fused([send(hop[u], T.OUT[:, 2 * W * ((u - a) % 3):2 * W * ((u - a) % 3) + 2 * W], T.HB[:, :], cs[u],
-                             T.sem.hb, topo) for u in range(3)], local_sem=T.sem.loc)
-    nloc += 12
-    g.wait_ge(T.sem.gv2, 2)
+    nloc += to_ports(T.OUT, G, T.HB, T.sem.hb)
+    g.wait_ge(T.sem.gv2, 1)
     g.wait_ge(T.sem.gs2, 1)
-    nloc += direct(lambda k: T.OUT[:, (6 + k) * W:(7 + k) * W], T.Z[:, zs:zs + W], T.sem.arr2)
+    nloc += straight(gathered, T.Z[:, zs:zs + W], T.sem.arr2)
+    g.wait_ge(T.sem.gs3, 1)
+    nloc += to_die(gathered, T.HB, T.sem.hb)
 
-    vec.wait_ge(T.sem.io3, 1)
     v(vec.tensor_scalar(T.A[:, :], T.I0[:, :], T.SM[:, 0:1], None, add))
     v(vec.tensor_scalar(T.RHO[:, :], T.A[:, :], COLS - 1, None, band))
-    v(vec.tensor_scalar(T.B3[:, :], T.RHO[:, :], 3, None, mult))
-    v(vec.tensor_scalar(T.BJ[:, :], T.B3[:, :], 9, None, shr))
-    v(vec.tensor_scalar(T.E6[:, :], T.BJ[:, :], 6, None, mult))
-    v(vec.tensor_scalar(T.H6[:, :], T.RHO[:, :], 1024, 6, ge, mult))
-    v(vec.tensor_tensor(T.F[:, :], T.E6[:, :], T.RHO[:, :], add))
-    v(vec.tensor_tensor(T.F2[:, :], T.F[:, :], T.H6[:, :], add))
-    v(vec.tensor_copy(T.L2[:, :], T.F2[:, :]))
+    v(vec.tensor_scalar(T.H4[:, :], T.RHO[:, :], COLS // 2, HW - HALF, ge, mult))
+    v(vec.tensor_tensor(T.F[:, :], T.H4[:, :], T.RHO[:, :], add))
+    v(vec.tensor_copy(T.L2[:, :], T.F[:, :]))
 
     g.scalar.wait_ge(T.sem.vc, n[0])
-    g.scalar.wait_ge(T.sem.gv2, 2)
-    vec.wait_ge(T.sem.gv2, 2)
     for q in (vec, g.scalar):
+        q.wait_ge(T.sem.own2, 16)
         q.wait_ge(T.sem.arr2, 40)
 
     def turn(b):

@@ -9,7 +9,11 @@ HALF = 1022
 HW = 6 * W
 NW = N * W
 K = G // 16
-LC = N * K
+KP = K + 1
+LC = N * KP
+GROUPS = ((0,), (1, 2))
+PLAN = (("relay", (4, 3)), ("straight", (0, 1)), ("straight", (2,)))
+HELPER = {4: 3, 3: 4}
 
 SCRATCH = {
     "XC": ("sbuf", [128, HW], "bfloat16"), "XS": ("sbuf", [128, HW], "bfloat16"),
@@ -18,22 +22,21 @@ SCRATCH = {
     "Z": ("sbuf", [128, NW], "bfloat16"),
     "YO": ("sbuf", [128, COLS], "bfloat16"),
     "HA": ("sbuf", [128, 2 * W], "bfloat16"), "HB": ("sbuf", [128, G + W], "bfloat16"),
-    "HH": ("sbuf", [128, 2], "int32"), "HF": ("sbuf", [128, 1], "float32"),
-    "SI": ("sbuf", [128, 128], "int32"), "SJ": ("sbuf", [128, 128], "int32"), "SEL": ("sbuf", [128, 128], "float32"),
-    "PI": ("sbuf", [128, 1], "int32"), "PJ": ("sbuf", [128, 1], "int32"),
-    "PM": ("sbuf", [128, 1], "float32"), "NPM": ("sbuf", [128, 1], "float32"),
-    "HI": ("sbuf", [128, 1], "int32"), "QI": ("sbuf", [128, 1], "int32"), "RI": ("sbuf", [128, 1], "int32"),
-    "SP": ("sbuf", [128, 1], "float32"), "SM": ("sbuf", [128, 1], "float32"),
-    "QW": ("sbuf", [128, 1], "float32"), "THR": ("sbuf", [128, 1], "float32"),
+    "HH": ("sbuf", [128, 2], "int32"), "QI": ("sbuf", [128, 1], "int32"), "RI": ("sbuf", [128, 1], "int32"),
+    "P": ("sbuf", [128, 1], "int32"), "HD": ("sbuf", [128, 128], "int32"), "SEL": ("sbuf", [128, 128], "float32"),
+    "K0": ("sbuf", [128, 1], "float32"), "KN": ("sbuf", [128, 1], "float32"), "KT": ("sbuf", [128, 1], "float32"),
+    "RH": ("sbuf", [128, 4], "float32"), "SM": ("sbuf", [128, 1], "float32"),
     "TA": ("sbuf", [128, LC], "int32"), "E": ("sbuf", [128, LC], "int32"),
     "M": ("sbuf", [128, LC], "int32"), "V": ("sbuf", [128, LC], "int32"),
-    "O": ("sbuf", [128, LC], "int32"), "R": ("sbuf", [128, LC], "int32"), "L1": ("sbuf", [128, LC + 8], "uint16"),
-    "I0": ("sbuf", [128, 128], "int32"), "A": ("sbuf", [128, 128], "int32"), "RHO": ("sbuf", [128, 128], "int32"),
+    "O": ("sbuf", [128, LC], "int32"), "R": ("sbuf", [128, LC], "int32"), "L1": ("sbuf", [128, LC], "uint16"),
+    "PF": ("sbuf", [128, 1], "float32"), "I0": ("sbuf", [128, 128], "int32"),
+    "C0": ("sbuf", [128, 128], "int32"), "A": ("sbuf", [128, 128], "int32"), "RHO": ("sbuf", [128, 128], "int32"),
     "H4": ("sbuf", [128, 128], "int32"), "F": ("sbuf", [128, 128], "int32"), "L2": ("sbuf", [128, 128], "uint16"),
     "ps": ("psum", [128, 8], "float32"),
 }
-SEMAPHORES = ["ldc", "lds", "own1", "own2", "ldh", "io1", "tab", "vc", "pe", "arr1", "arr2", "ha", "hb",
-              "loc", "gv1", "gv2", "gv3", "gs1", "gs2", "gs3", "y0", "y1", "y2", "y3", "st", "st2"]
+SEMAPHORES = ["ld0", "ld1", "lds", "own1", "own2", "ldh", "io1", "tab", "tab2", "sm", "l2", "vc", "pe",
+              "arr1", "arr2", "ha", "hb", "loc", "ga0", "ga1", "ga2", "go0", "go1", "go2", "gown",
+              "y0", "y1", "y2", "y3", "st", "st2"]
 
 
 def engines(mask):
@@ -42,6 +45,11 @@ def engines(mask):
 
 def bitmask(es):
     return sum(1 << e for e in es)
+
+
+def share(es, i, n):
+    m = len(es) // n
+    return es[m * i:m * i + m]
 
 
 def planes(T, topo):
@@ -76,7 +84,15 @@ def carriers(rank, T, topo, pl):
     chip = [c for c in range(topo.CHIPS * topo.CORES_PER_CHIP) if c != core and topo.chip(c) == topo.chip(core)]
     chip = [c for c in chip if topo.die(c) != topo.die(core)] + [c for c in chip if topo.die(c) == topo.die(core)]
     port = [c for c in chip if topo.may_write(c, far)][:3]
-    return port + [c for c in chip if c not in port][:1]
+    return port + [c for c in chip if c not in port][:3]
+
+
+def engine_sets(rank, T, topo, pl):
+    core = T.cores[rank]
+    off = engines(topo.mask(core, T.cores[destinations(rank, pl)[1][0]]))
+    on = engines(topo.mask(core, carriers(rank, T, topo, pl)[0]))
+    order = [e for e in on if e not in off] + off[::-1]
+    return off, order, order[:8]
 
 
 def send(mask_engines, src, out, to, sem, topo):
@@ -86,44 +102,84 @@ def send(mask_engines, src, out, to, sem, topo):
 
 
 def table(g, rank, u, T, pl):
-    if u == 0:
-        g.iota(T.TA[:, :], [[0, N], [16, K]], start(rank, pl), 1).then_inc(T.sem.io1, 1)
-        return T.TA[:, :], 1
-    if u == 3:
-        g.iota(T.I0[:, :], [[16, 128]], 0, 1).then_inc(T.sem.io1, 1)
-        return T.I0[:, :], 1
+    if u in (0, 5):
+        out = T.TA[:, 0:6 * KP] if u == 0 else T.TA[:, 6 * KP:LC]
+        g.iota(out, [[0, 6], [16, KP]], start(rank, pl), 1).then_inc(T.sem.io1, 1)
+        return out, 1
+    if u in (3, 4):
+        c = 64 * (u - 3)
+        g.iota(T.C0[:, c:c + 64], [[16, 64]], 16 * c, 0).then_inc(T.sem.io1, 1)
+        return T.C0[:, c:c + 64], 1
     n = i = 0
-    lst, c = destinations(rank, pl)[u - 1], 6 * K * (u - 1)
+    lst, c = destinations(rank, pl)[u - 1], 6 * KP * (u - 1)
     while i < len(lst):
         j = i + 1
         while j < len(lst) and lst[j] - lst[j - 1] == lst[i + 1] - lst[i]:
             j += 1
         step = lst[i + 1] - lst[i] if j > i + 1 else 0
-        g.iota(T.E[:, c + i * K:c + j * K], [[step * W, j - i], [16, K]], lst[i] * W, 1).then_inc(T.sem.io1, 1)
+        g.iota(T.E[:, c + i * KP:c + j * KP], [[step * W, j - i], [16, KP]], lst[i] * W, 1).then_inc(T.sem.io1, 1)
         n += 1
         i = j
-    return T.E[:, c:c + 6 * K], n
+    return T.E[:, c:c + 6 * KP], n
 
 
 def carrier_program(g, core, rank, u, T, topo, pl):
     half, a = place(rank, pl)
-    v = (u - a) % 3
-    to = [pl[1 - half][2 * v], pl[1 - half][2 * v + 1]] if u < 3 else [destinations(rank, pl)[1][4]]
     zs = zslot(rank, pl)
+    _, order, inner = engine_sets(rank, T, topo, pl)
+    if u < 3:
+        v = (u - a) % 3
+        to = [pl[1 - half][2 * v], pl[1 - half][2 * v + 1]]
+        m = [len(order) // len(gr) for gr in GROUPS if u in gr][0]
+    else:
+        k, m = [(k, len(inner) // len(ks)) for kind, ks in PLAN for k in ks if kind == "relay" and HELPER[k] == u][0]
+        to = [destinations(rank, pl)[1][k]]
     es = engines(topo.mask(core, T.cores[to[0]]))
-    h = len(es) // len(to)
     buf, n = table(g, rank, u, T, pl)
     g.wait_ge(T.sem.io1, n)
-    rid, pid, _ = topo.addr(T.cores[rank])
+    rid, pid, _ = topo.addr(T.cores[rank] if u < 3 else carriers(rank, T, topo, pl)[5])
     g.remote_dma(buf, buf, T.sem.tab, T.sem.loc, pid, rid, bitmask(es))
-    n = len(es)
     for sem, buf, step, out, arr in ((T.sem.ha, T.HA, W, T.W[:, rank * W:(rank + 1) * W], T.sem.arr1),
                                      (T.sem.hb, T.HB, G, T.Z[:, zs:zs + W], T.sem.arr2)):
-        g.wait_ge(sem, 4 if u < 3 else 8)
-        g.remote_dma_fused([send(es[i * h:(i + 1) * h], buf[:, i * step:i * step + W], out, T.cores[to[i]], arr, topo)
+        g.wait_ge(sem, m)
+        g.remote_dma_fused([send(share(es, i, len(to)), buf[:, i * step:i * step + W], out, T.cores[to[i]], arr, topo)
                             for i in range(len(to))], local_sem=T.sem.loc)
-        n += len(es)
-    g.wait_ge(T.sem.loc, n)
+    g.wait_ge(T.sem.loc, 3 * len(es))
+
+
+def chain(queue, sem, n):
+    def run(*ins):
+        for i in ins:
+            i.then_inc(sem, 1)
+            n[0] += 1
+        queue.wait_ge(sem, n[0])
+    return run
+
+
+def list_program(g, core, rank, cs, T, topo, pl):
+    add, mult, ge, band = AluOpType.add, AluOpType.mult, AluOpType.is_ge, AluOpType.bitwise_and
+    rank_core = T.cores[rank]
+    es = engines(topo.mask(core, rank_core))[:8]
+    rid, pid, _ = topo.addr(rank_core)
+    buf, n = table(g, rank, 5, T, pl)
+    g.wait_ge(T.sem.io1, n)
+    g.remote_dma(buf, buf, T.sem.tab, T.sem.loc, pid, rid, bitmask(es))
+    vec = g.vector
+    n = [0]
+    v = chain(vec, T.sem.vc, n)
+    vec.wait_ge(T.sem.tab2, len(engines(topo.mask(rank_core, core))))
+    v(vec.tensor_copy(T.PF[:, 0:1], T.P[:, 0:1]))
+    vec.wait_ge(T.sem.tab, 2 * len(engines(topo.mask(cs[3], T.cores[destinations(rank, pl)[1][0]]))))
+    v(vec.tensor_scalar(T.I0[:, :], T.C0[:, :], T.PF[:, 0:1], None, add))
+    vec.wait_ge(T.sem.sm, 8)
+    v(vec.tensor_scalar(T.A[:, :], T.I0[:, :], T.SM[:, 0:1], None, add))
+    v(vec.tensor_scalar(T.RHO[:, :], T.A[:, :], COLS - 1, None, band))
+    v(vec.tensor_scalar(T.H4[:, :], T.RHO[:, :], COLS // 2, HW - HALF, ge, mult))
+    v(vec.tensor_tensor(T.F[:, :], T.H4[:, :], T.RHO[:, :], add))
+    v(vec.tensor_copy(T.L2[:, :], T.F[:, :]))
+    g.wait_ge(T.sem.vc, n[0])
+    g.remote_dma(T.L2[:, :], T.L2[:, :], T.sem.l2, T.sem.loc, pid, rid, bitmask(es))
+    g.wait_ge(T.sem.loc, 2 * len(es))
 
 
 def rank_program(g, core, T, topo):
@@ -133,148 +189,132 @@ def rank_program(g, core, T, topo):
         for r in range(N):
             if topo.chip(T.cores[r]) == topo.chip(core):
                 cs = carriers(r, T, topo, pl)
-                if core in cs:
+                if core == cs[5]:
+                    list_program(g, core, r, cs, T, topo, pl)
+                elif core in cs:
                     carrier_program(g, core, r, cs.index(core), T, topo, pl)
         return
     half, a = place(rank, pl)
     others = destinations(rank, pl)[1][:5]
     cs = carriers(rank, T, topo, pl)
-    off = engines(topo.mask(core, T.cores[others[0]]))
-    on = engines(topo.mask(core, cs[0]))
-    order = [e for e in on if e not in off] + off[::-1]
-    hop = [order[4 * u:4 * u + 4] for u in range(3)]
+    pair = [(u - a) % 3 for u in range(3)]
+    off, order, inner = engine_sets(rank, T, topo, pl)
     add, mult, lt, ge, eq = AluOpType.add, AluOpType.mult, AluOpType.is_lt, AluOpType.is_ge, AluOpType.is_equal
     shr, band, low = AluOpType.arith_shift_right, AluOpType.bitwise_and, AluOpType.min
     copy = ActivationFunctionType.Copy
     zs, s0 = zslot(rank, pl), start(rank, pl)
+    landed = 6 * 4 + sum(8 // len(ks) if kind == "straight" else 8 for kind, ks in PLAN for k in ks)
 
     lo_c, lo_s = HALF * (1 - half), HALF * half
-    g.sync.dma_start(T.XC[:, :], T.x[:, lo_c:lo_c + HW]).then_inc(T.sem.ldc, 16)
+    for i, group in enumerate(GROUPS):
+        for u in group:
+            c = 2 * W * pair[u]
+            g.sync.dma_start(T.XC[:, c:c + 2 * W], T.x[:, lo_c + c:lo_c + c + 2 * W]).then_inc(T.sem["ld%d" % i], 16)
     g.sync.dma_start(T.XS[:, :], T.x[:, lo_s:lo_s + HW]).then_inc(T.sem.lds, 16)
     g.sync.dma_start(T.W[:, rank * W:(rank + 1) * W], T.x[:, s0:s0 + W]).then_inc(T.sem.own1, 16)
     g.scalar.dma_start(T.HH[0:16, 0:2], T.hh[:, :]).then_inc(T.sem.ldh, 16)
-    g.iota(T.SI[0:16, :], [[1, 128]], 0, -16).then_inc(T.sem.io1, 1)
-    g.iota(T.PI[:, 0:1], [[1, 1]], 0, 1).then_inc(T.sem.io1, 1)
 
     nloc = 0
 
-    def to_ports(src, step, out, sem):
-        g.remote_dma_fused([send(hop[u], src[:, 2 * step * ((u - a) % 3):2 * step * ((u - a) % 3) + step + W], out[:, :],
-                                 cs[u], sem, topo) for u in range(3)], local_sem=T.sem.loc)
-        return 12
+    def to_list_core(buf, sem, es):
+        rid, pid, _ = topo.addr(cs[5])
+        g.remote_dma(buf, buf, sem, T.sem.loc, pid, rid, bitmask(es))
+        return len(es)
+    g.iota(T.P[:, 0:1], [[1, 1]], 0, 1).then_inc(T.sem.io1, 1)
+    g.iota(T.HD[0:16, :], [[1, 8], [0, 16]], 0, -1).then_inc(T.sem.io1, 1)
+    g.wait_ge(T.sem.io1, 2)
+    nloc += to_list_core(T.P[:, 0:1], T.sem.tab2, order)
 
-    def straight(src, out, arr):
-        g.remote_dma_fused([send(off[2 * k:2 * k + 2], src(k), out, T.cores[others[k]], arr, topo) for k in range(4)],
-                           local_sem=T.sem.loc)
-        return 8
+    def to_ports(waits, src, step, out, sem):
+        n = 0
+        for group, w in zip(GROUPS, waits):
+            for s, m in w:
+                g.wait_ge(s, m)
+            g.remote_dma_fused([send(share(order, i, len(group)), src[:, 2 * step * pair[u]:2 * step * pair[u] + step + W],
+                                     out[:, :], cs[u], sem, topo) for i, u in enumerate(group)], local_sem=T.sem.loc)
+            n += len(order)
+        return n
 
-    def to_die(src, out, sem):
-        rid, pid, _ = topo.addr(cs[3])
-        g.remote_dma(out[:, 0:W], src(4), sem, T.sem.loc, pid, rid, bitmask(order[:8]))
-        return 8
+    def own_plane(waits, src, out, arr, buf, sem):
+        n = 0
+        for (kind, ks), w in zip(PLAN, waits):
+            for s, m in w:
+                g.wait_ge(s, m)
+            if kind == "straight":
+                g.remote_dma_fused([send(share(off, i, len(ks)), src(k), out, T.cores[others[k]], arr, topo)
+                                    for i, k in enumerate(ks)], local_sem=T.sem.loc)
+            else:
+                g.remote_dma_fused([send(share(inner, i, len(ks)), src(k), buf[:, 0:W], cs[HELPER[k]], sem, topo)
+                                    for i, k in enumerate(ks)], local_sem=T.sem.loc)
+            n += 8
+        return n
 
     def piece(k):
         b = place(others[k], pl)[1]
         return T.XS[:, W * b:W * b + W]
-    g.wait_ge(T.sem.ldc, 16)
-    nloc += to_ports(T.XC, W, T.HA, T.sem.ha)
-    g.wait_ge(T.sem.lds, 16)
-    nloc += straight(piece, T.W[:, rank * W:(rank + 1) * W], T.sem.arr1)
-    nloc += to_die(piece, T.HA, T.sem.ha)
+    nloc += to_ports([[(T.sem["ld%d" % i], 16 * len(gr))] for i, gr in enumerate(GROUPS)], T.XC, W, T.HA, T.sem.ha)
+    nloc += own_plane([[(T.sem.lds, 16)], [], []], piece, T.W[:, rank * W:(rank + 1) * W], T.sem.arr1, T.HA, T.sem.ha)
 
     vec = g.vector
     n = [0]
-
-    def v(ins):
-        ins.then_inc(T.sem.vc, 1)
-        n[0] += 1
-        vec.wait_ge(T.sem.vc, n[0])
+    v = chain(vec, T.sem.vc, n)
     vec.wait_ge(T.sem.io1, 2)
-    v(vec.tensor_scalar(T.SJ[0:16, :], T.SI[0:16, :], 4, None, shr))
-    v(vec.tensor_scalar(T.SEL[0:16, :], T.SJ[0:16, :], 0, None, eq))
-    v(vec.tensor_scalar(T.PJ[:, 0:1], T.PI[:, 0:1], 4, None, shr))
-    v(vec.tensor_scalar(T.PM[:, 0:1], T.PJ[:, 0:1], 16, None, mult))
-    v(vec.tensor_scalar(T.NPM[:, 0:1], T.PJ[:, 0:1], -16, None, mult))
+    v(vec.tensor_scalar(T.SEL[0:16, :], T.HD[0:16, :], 0, None, eq),
+      vec.tensor_scalar(T.K0[0:16, 0:1], T.P[0:16, 0:1], 16, None, mult),
+      vec.tensor_scalar(T.KN[0:16, 0:1], T.P[0:16, 0:1], -16, None, mult),
+      vec.tensor_scalar(T.KT[0:16, 0:1], T.P[0:16, 0:1], 16, NW, mult, add))
     vec.wait_ge(T.sem.ldh, 16)
-    v(vec.tensor_copy(T.HF[0:16, 0:1], T.HH[0:16, 0:1]))
+    v(vec.tensor_scalar(T.QI[0:16, 0:1], T.HH[0:16, 0:1], 11, None, shr),
+      vec.tensor_scalar(T.RI[0:16, 0:1], T.HH[0:16, 0:1], COLS - 1, None, band))
+    v(vec.tensor_scalar(T.RH[0:16, 0:1], T.RI[0:16, 0:1], T.K0[0:16, 0:1], None, add),
+      vec.tensor_scalar(T.RH[0:16, 1:2], T.QI[0:16, 0:1], -W, T.KT[0:16, 0:1], mult, add),
+      vec.tensor_scalar(T.RH[0:16, 2:3], T.QI[0:16, 0:1], W, T.KN[0:16, 0:1], mult, add),
+      vec.tensor_scalar(T.RH[0:16, 3:4], T.RI[0:16, 0:1], T.KN[0:16, 0:1], None, add))
     g.tensor.wait_ge(T.sem.vc, n[0])
-    g.tensor.matmul(T.ps[:, 0:1], T.SEL[0:16, :], T.HF[0:16, 0:1], True, True).then_inc(T.sem.pe, 1)
+    g.tensor.matmul(T.ps[:, 0:4], T.SEL[0:16, :], T.RH[0:16, 0:4], True, True).then_inc(T.sem.pe, 1)
+    vec.wait_ge(T.sem.tab, 3 * len(off) + 8)
     vec.wait_ge(T.sem.pe, 1)
-    v(vec.tensor_copy(T.HI[:, 0:1], T.ps[:, 0:1]))
-    v(vec.tensor_scalar(T.QI[:, 0:1], T.HI[:, 0:1], 11, None, shr))
-    v(vec.tensor_scalar(T.RI[:, 0:1], T.HI[:, 0:1], COLS - 1, None, band))
-    v(vec.tensor_scalar(T.SP[:, 0:1], T.RI[:, 0:1], T.PM[:, 0:1], None, add))
-    v(vec.tensor_scalar(T.SM[:, 0:1], T.RI[:, 0:1], T.NPM[:, 0:1], None, add))
-    v(vec.tensor_scalar(T.QW[:, 0:1], T.QI[:, 0:1], W, T.NPM[:, 0:1], mult, add))
-    v(vec.tensor_scalar(T.THR[:, 0:1], T.QW[:, 0:1], -1, NW, mult, add))
-    vec.wait_ge(T.sem.tab, 4 * len(off))
-    v(vec.tensor_scalar(T.M[:, :], T.TA[:, :], T.SP[:, 0:1], W, lt, mult))
+    v(vec.tensor_scalar(T.M[:, :], T.TA[:, :], T.ps[:, 0:1], W, lt, mult))
     v(vec.tensor_tensor(T.V[:, :], T.E[:, :], T.M[:, :], add))
-    v(vec.tensor_scalar(T.O[:, :], T.V[:, :], T.THR[:, 0:1], -NW, ge, mult))
+    v(vec.tensor_scalar(T.O[:, :], T.V[:, :], T.ps[:, 1:2], -NW, ge, mult))
     v(vec.tensor_tensor(T.R[:, :], T.V[:, :], T.O[:, :], add))
-    at = {}
-    c = 0
-    for lo, hi in ((0, 3), (3, 6), (6, 11), (11, 12)):
-        vec.tensor_scalar(T.L1[:, c:c + (hi - lo) * K], T.R[:, lo * K:hi * K], T.QW[:, 0:1], NW - 1, add,
-                          low).then_inc(T.sem.vc, 1)
-        for i in range(lo, hi):
-            at[i] = c + (i - lo) * K
-        c += (hi - lo) * K
-        c += c % 2
-        n[0] += 1
-    vec.wait_ge(T.sem.vc, n[0])
+    v(vec.tensor_scalar(T.L1[:, :], T.R[:, :], T.ps[:, 2:3], NW - 1, add, low),
+      vec.tensor_copy(T.SM[:, 0:1], T.ps[:, 3:4]))
+    g.wait_ge(T.sem.vc, n[0])
+    nloc += to_list_core(T.SM[:, 0:1], T.sem.sm, inner)
 
     g.scalar.wait_ge(T.sem.vc, n[0])
     for q in (vec, g.scalar):
         q.wait_ge(T.sem.own1, 16)
-        q.wait_ge(T.sem.arr1, 40)
-
-    def pick(lo, hi):
-        return T.W[:, :].indirect(T.L1[:, at[lo]:at[lo] + (hi - lo) * K])
-    for lo, hi, sem in ((0, 3, T.sem.gv1), (6, 8, T.sem.gv2), (11, 12, T.sem.gv3)):
-        vec.tensor_copy(T.OUT[:, lo * G:hi * G], pick(lo, hi)).then_inc(sem, 1)
-    for lo, hi, sem in ((3, 6, T.sem.gs1), (8, 10, T.sem.gs2), (10, 11, T.sem.gs3)):
-        g.scalar.activation(T.OUT[:, lo * G:hi * G], pick(lo, hi), copy).then_inc(sem, 1)
-    g.sync.wait_ge(T.sem.gv3, 1)
+        q.wait_ge(T.sem.arr1, landed)
+    queue = [(2 * pair[u] + e, T.sem["ga%d" % u]) for u in range(3) for e in range(2)]
+    queue += [(6 + k, T.sem["go%d" % i]) for i, (kind, ks) in enumerate(PLAN) for k in ks] + [(11, T.sem.gown)]
+    for e, (i, sem) in enumerate(queue):
+        out, src = T.OUT[:, i * G:(i + 1) * G], T.W[:, :].indirect(T.L1[:, i * KP:i * KP + K])
+        ins = g.scalar.activation(out, src, copy) if e % 2 else vec.tensor_copy(out, src)
+        ins.then_inc(sem, 1)
+    g.sync.wait_ge(T.sem.gown, 1)
     g.sync.dma_start(T.Z[:, zs:zs + W], T.OUT[:, 11 * G:11 * G + W]).then_inc(T.sem.own2, 16)
 
     def gathered(k):
         return T.OUT[:, (6 + k) * G:(6 + k) * G + W]
-    g.wait_ge(T.sem.gv1, 1)
-    g.wait_ge(T.sem.gs1, 1)
-    nloc += to_ports(T.OUT, G, T.HB, T.sem.hb)
-    g.wait_ge(T.sem.gv2, 1)
-    g.wait_ge(T.sem.gs2, 1)
-    nloc += straight(gathered, T.Z[:, zs:zs + W], T.sem.arr2)
-    g.wait_ge(T.sem.gs3, 1)
-    nloc += to_die(gathered, T.HB, T.sem.hb)
+    nloc += to_ports([[(T.sem["ga%d" % u], 2) for u in gr] for gr in GROUPS], T.OUT, G, T.HB, T.sem.hb)
+    nloc += own_plane([[(T.sem["go%d" % i], len(ks))] for i, (kind, ks) in enumerate(PLAN)], gathered,
+                      T.Z[:, zs:zs + W], T.sem.arr2, T.HB, T.sem.hb)
 
-    v(vec.tensor_scalar(T.A[:, :], T.I0[:, :], T.SM[:, 0:1], None, add))
-    v(vec.tensor_scalar(T.RHO[:, :], T.A[:, :], COLS - 1, None, band))
-    v(vec.tensor_scalar(T.H4[:, :], T.RHO[:, :], COLS // 2, HW - HALF, ge, mult))
-    v(vec.tensor_tensor(T.F[:, :], T.H4[:, :], T.RHO[:, :], add))
-    v(vec.tensor_copy(T.L2[:, :], T.F[:, :]))
-
-    g.scalar.wait_ge(T.sem.vc, n[0])
     for q in (vec, g.scalar):
+        q.wait_ge(T.sem.l2, 8)
         q.wait_ge(T.sem.own2, 16)
-        q.wait_ge(T.sem.arr2, 40)
-
-    def turn(b):
-        return T.YO[:, 512 * b:512 * b + 512], T.Z[:, :].indirect(T.L2[:, 32 * b:32 * b + 32])
-    out, src = turn(0)
-    vec.tensor_copy(out, src).then_inc(T.sem.y0, 1)
-    out, src = turn(1)
-    vec.tensor_copy(out, src).then_inc(T.sem.y1, 1)
-    out, src = turn(2)
-    g.scalar.activation(out, src, copy).then_inc(T.sem.y2, 1)
-    out, src = turn(3)
-    g.scalar.activation(out, src, copy).then_inc(T.sem.y3, 1)
-    for b, sem in ((0, T.sem.y0), (2, T.sem.y2), (1, T.sem.y1)):
-        g.sync.wait_ge(sem, 1)
-        g.sync.dma_start(T.y[:, 512 * b:512 * b + 512], T.YO[:, 512 * b:512 * b + 512]).then_inc(T.sem.st, 16)
-    g.scalar.wait_ge(T.sem.y3, 1)
-    g.scalar.dma_start(T.y[:, 1536:2048], T.YO[:, 1536:2048]).then_inc(T.sem.st2, 16)
+        q.wait_ge(T.sem.arr2, landed)
+    blocks = [512 * b + COLS // 2 * e for b in range(2) for e in range(2)]
+    for b, c in enumerate(blocks):
+        out, src = T.YO[:, c:c + 512], T.Z[:, :].indirect(T.L2[:, c // 16:c // 16 + 32])
+        ins = g.scalar.activation(out, src, copy) if b % 2 else vec.tensor_copy(out, src)
+        ins.then_inc(T.sem["y%d" % b], 1)
+    for b, c in enumerate(blocks):
+        q, st = (g.scalar, T.sem.st2) if b == 3 else (g.sync, T.sem.st)
+        q.wait_ge(T.sem["y%d" % b], 1)
+        q.dma_start(T.y[:, c:c + 512], T.YO[:, c:c + 512]).then_inc(st, 16)
     g.sync.wait_ge(T.sem.st, 48)
     g.scalar.wait_ge(T.sem.st2, 16)
     g.wait_ge(T.sem.loc, nloc)

from concourse.bass import DstId, RemoteDMATransfer
from concourse.mybir import AluOpType, ActivationFunctionType

N = 12
COLS = 2048
W = 171
G = 176
HALF = 1022
HW = 6 * W
NW = N * W
K = G // 16
KP = K + 1
LC = N * KP
GROUPS = ((0,), (1, 2))
PLAN = (("relay", (4, 3)), ("straight", (0, 1)), ("straight", (2,)))
HELPER = {4: 3, 3: 4}

SCRATCH = {
    "XC": ("sbuf", [128, HW], "bfloat16"), "XS": ("sbuf", [128, HW], "bfloat16"),
    "W": ("sbuf", [128, NW], "bfloat16"),
    "OUT": ("sbuf", [128, N * G], "bfloat16"),
    "Z": ("sbuf", [128, NW], "bfloat16"),
    "YO": ("sbuf", [128, COLS], "bfloat16"),
    "HA": ("sbuf", [128, 2 * W], "bfloat16"), "HB": ("sbuf", [128, G + W], "bfloat16"),
    "HH": ("sbuf", [128, 2], "int32"), "QI": ("sbuf", [128, 1], "int32"), "RI": ("sbuf", [128, 1], "int32"),
    "P": ("sbuf", [128, 1], "int32"), "HD": ("sbuf", [128, 128], "int32"), "SEL": ("sbuf", [128, 128], "float32"),
    "K0": ("sbuf", [128, 1], "float32"), "KN": ("sbuf", [128, 1], "float32"), "KT": ("sbuf", [128, 1], "float32"),
    "RH": ("sbuf", [128, 4], "float32"), "SM": ("sbuf", [128, 1], "float32"),
    "TA": ("sbuf", [128, LC], "int32"), "E": ("sbuf", [128, LC], "int32"),
    "M": ("sbuf", [128, LC], "int32"), "V": ("sbuf", [128, LC], "int32"),
    "O": ("sbuf", [128, LC], "int32"), "R": ("sbuf", [128, LC], "int32"), "L1": ("sbuf", [128, LC], "uint16"),
    "PF": ("sbuf", [128, 1], "float32"), "I0": ("sbuf", [128, 128], "int32"),
    "C0": ("sbuf", [128, 128], "int32"), "A": ("sbuf", [128, 128], "int32"), "RHO": ("sbuf", [128, 128], "int32"),
    "H4": ("sbuf", [128, 128], "int32"), "F": ("sbuf", [128, 128], "int32"), "L2": ("sbuf", [128, 128], "uint16"),
    "ps": ("psum", [128, 8], "float32"),
}
SEMAPHORES = ["ld0", "ld1", "lds", "own1", "own2", "ldh", "io1", "tab", "tab2", "sm", "l2", "vc", "pe",
              "arr1", "arr2", "ha", "hb", "loc", "ga0", "ga1", "ga2", "go0", "go1", "go2", "gown",
              "y0", "y1", "y2", "y3", "st", "st2"]


def engines(mask):
    return [e for e in range(mask.bit_length()) if (mask >> e) & 1]


def bitmask(es):
    return sum(1 << e for e in es)


def share(es, i, n):
    m = len(es) // n
    return es[m * i:m * i + m]


def planes(T, topo):
    c0 = topo.chip(T.cores[0])
    a = [r for r in range(N) if r == 0 or topo.same_plane(c0, topo.chip(T.cores[r]))]
    return [a, [r for r in range(N) if r not in a]]


def place(r, pl):
    half = 0 if r in pl[0] else 1
    return half, pl[half].index(r)


def start(r, pl):
    half, b = place(r, pl)
    return HALF * half + W * b


def zslot(r, pl):
    half, b = place(r, pl)
    return HW * half + W * b


def destinations(rank, pl):
    half, a = place(rank, pl)
    return pl[1 - half], [pl[half][(a + k) % 6] for k in range(1, 6)] + [rank]


def carriers(rank, T, topo, pl):
    core = T.cores[rank]
    far = T.cores[pl[1 - place(rank, pl)[0]][0]]
    chip = [c for c in range(topo.CHIPS * topo.CORES_PER_CHIP) if c != core and topo.chip(c) == topo.chip(core)]
    chip = [c for c in chip if topo.die(c) != topo.die(core)] + [c for c in chip if topo.die(c) == topo.die(core)]
    port = [c for c in chip if topo.may_write(c, far)][:3]
    return port + [c for c in chip if c not in port][:3]


def engine_sets(rank, T, topo, pl):
    core = T.cores[rank]
    off = engines(topo.mask(core, T.cores[destinations(rank, pl)[1][0]]))
    on = engines(topo.mask(core, carriers(rank, T, topo, pl)[0]))
    order = [e for e in on if e not in off] + off[::-1]
    return off, order, order[:8]


def send(mask_engines, src, out, to, sem, topo):
    rid, pid, _ = topo.addr(to)
    return RemoteDMATransfer(dst_ids=[DstId(rid=rid, pnc=pid)], dma_engine_mask=bitmask(mask_engines), remote_sem=sem,
                             src=src, dst=out)


def table(g, rank, u, T, pl):
    if u in (0, 5):
        out = T.TA[:, 0:6 * KP] if u == 0 else T.TA[:, 6 * KP:LC]
        g.iota(out, [[0, 6], [16, KP]], start(rank, pl), 1).then_inc(T.sem.io1, 1)
        return out, 1
    if u in (3, 4):
        c = 64 * (u - 3)
        g.iota(T.C0[:, c:c + 64], [[16, 64]], 16 * c, 0).then_inc(T.sem.io1, 1)
        return T.C0[:, c:c + 64], 1
    n = i = 0
    lst, c = destinations(rank, pl)[u - 1], 6 * KP * (u - 1)
    while i < len(lst):
        j = i + 1
        while j < len(lst) and lst[j] - lst[j - 1] == lst[i + 1] - lst[i]:
            j += 1
        step = lst[i + 1] - lst[i] if j > i + 1 else 0
        g.iota(T.E[:, c + i * KP:c + j * KP], [[step * W, j - i], [16, KP]], lst[i] * W, 1).then_inc(T.sem.io1, 1)
        n += 1
        i = j
    return T.E[:, c:c + 6 * KP], n


def carrier_program(g, core, rank, u, T, topo, pl):
    half, a = place(rank, pl)
    zs = zslot(rank, pl)
    _, order, inner = engine_sets(rank, T, topo, pl)
    if u < 3:
        v = (u - a) % 3
        to = [pl[1 - half][2 * v], pl[1 - half][2 * v + 1]]
        m = [len(order) // len(gr) for gr in GROUPS if u in gr][0]
    else:
        k, m = [(k, len(inner) // len(ks)) for kind, ks in PLAN for k in ks if kind == "relay" and HELPER[k] == u][0]
        to = [destinations(rank, pl)[1][k]]
    es = engines(topo.mask(core, T.cores[to[0]]))
    buf, n = table(g, rank, u, T, pl)
    g.wait_ge(T.sem.io1, n)
    rid, pid, _ = topo.addr(T.cores[rank] if u < 3 else carriers(rank, T, topo, pl)[5])
    g.remote_dma(buf, buf, T.sem.tab, T.sem.loc, pid, rid, bitmask(es))
    for sem, buf, step, out, arr in ((T.sem.ha, T.HA, W, T.W[:, rank * W:(rank + 1) * W], T.sem.arr1),
                                     (T.sem.hb, T.HB, G, T.Z[:, zs:zs + W], T.sem.arr2)):
        g.wait_ge(sem, m)
        g.remote_dma_fused([send(share(es, i, len(to)), buf[:, i * step:i * step + W], out, T.cores[to[i]], arr, topo)
                            for i in range(len(to))], local_sem=T.sem.loc)
    g.wait_ge(T.sem.loc, 3 * len(es))


def chain(queue, sem, n):
    def run(*ins):
        for i in ins:
            i.then_inc(sem, 1)
            n[0] += 1
        queue.wait_ge(sem, n[0])
    return run


def list_program(g, core, rank, cs, T, topo, pl):
    add, mult, ge, band = AluOpType.add, AluOpType.mult, AluOpType.is_ge, AluOpType.bitwise_and
    rank_core = T.cores[rank]
    es = engines(topo.mask(core, rank_core))[:8]
    rid, pid, _ = topo.addr(rank_core)
    buf, n = table(g, rank, 5, T, pl)
    g.wait_ge(T.sem.io1, n)
    g.remote_dma(buf, buf, T.sem.tab, T.sem.loc, pid, rid, bitmask(es))
    vec = g.vector
    n = [0]
    v = chain(vec, T.sem.vc, n)
    vec.wait_ge(T.sem.tab2, len(engines(topo.mask(rank_core, core))))
    v(vec.tensor_copy(T.PF[:, 0:1], T.P[:, 0:1]))
    vec.wait_ge(T.sem.tab, 2 * len(engines(topo.mask(cs[3], T.cores[destinations(rank, pl)[1][0]]))))
    v(vec.tensor_scalar(T.I0[:, :], T.C0[:, :], T.PF[:, 0:1], None, add))
    vec.wait_ge(T.sem.sm, 8)
    v(vec.tensor_scalar(T.A[:, :], T.I0[:, :], T.SM[:, 0:1], None, add))
    v(vec.tensor_scalar(T.RHO[:, :], T.A[:, :], COLS - 1, None, band))
    v(vec.tensor_scalar(T.H4[:, :], T.RHO[:, :], COLS // 2, HW - HALF, ge, mult))
    v(vec.tensor_tensor(T.F[:, :], T.H4[:, :], T.RHO[:, :], add))
    v(vec.tensor_copy(T.L2[:, :], T.F[:, :]))
    g.wait_ge(T.sem.vc, n[0])
    g.remote_dma(T.L2[:, :], T.L2[:, :], T.sem.l2, T.sem.loc, pid, rid, bitmask(es))
    g.wait_ge(T.sem.loc, 2 * len(es))


def rank_program(g, core, T, topo):
    pl = planes(T, topo)
    rank = T.rank_of(core)
    if rank is None:
        for r in range(N):
            if topo.chip(T.cores[r]) == topo.chip(core):
                cs = carriers(r, T, topo, pl)
                if core == cs[5]:
                    list_program(g, core, r, cs, T, topo, pl)
                elif core in cs:
                    carrier_program(g, core, r, cs.index(core), T, topo, pl)
        return
    half, a = place(rank, pl)
    others = destinations(rank, pl)[1][:5]
    cs = carriers(rank, T, topo, pl)
    pair = [(u - a) % 3 for u in range(3)]
    off, order, inner = engine_sets(rank, T, topo, pl)
    add, mult, lt, ge, eq = AluOpType.add, AluOpType.mult, AluOpType.is_lt, AluOpType.is_ge, AluOpType.is_equal
    shr, band, low = AluOpType.arith_shift_right, AluOpType.bitwise_and, AluOpType.min
    copy = ActivationFunctionType.Copy
    zs, s0 = zslot(rank, pl), start(rank, pl)
    landed = 6 * 4 + sum(8 // len(ks) if kind == "straight" else 8 for kind, ks in PLAN for k in ks)

    lo_c, lo_s = HALF * (1 - half), HALF * half
    for i, group in enumerate(GROUPS):
        for u in group:
            c = 2 * W * pair[u]
            g.sync.dma_start(T.XC[:, c:c + 2 * W], T.x[:, lo_c + c:lo_c + c + 2 * W]).then_inc(T.sem["ld%d" % i], 16)
    g.sync.dma_start(T.XS[:, :], T.x[:, lo_s:lo_s + HW]).then_inc(T.sem.lds, 16)
    g.sync.dma_start(T.W[:, rank * W:(rank + 1) * W], T.x[:, s0:s0 + W]).then_inc(T.sem.own1, 16)
    g.scalar.dma_start(T.HH[0:16, 0:2], T.hh[:, :]).then_inc(T.sem.ldh, 16)

    nloc = 0

    def to_list_core(buf, sem, es):
        rid, pid, _ = topo.addr(cs[5])
        g.remote_dma(buf, buf, sem, T.sem.loc, pid, rid, bitmask(es))
        return len(es)
    g.iota(T.P[:, 0:1], [[1, 1]], 0, 1).then_inc(T.sem.io1, 1)
    g.iota(T.HD[0:16, :], [[1, 8], [0, 16]], 0, -1).then_inc(T.sem.io1, 1)
    g.wait_ge(T.sem.io1, 2)
    nloc += to_list_core(T.P[:, 0:1], T.sem.tab2, order)

    def to_ports(waits, src, step, out, sem):
        n = 0
        for group, w in zip(GROUPS, waits):
            for s, m in w:
                g.wait_ge(s, m)
            g.remote_dma_fused([send(share(order, i, len(group)), src[:, 2 * step * pair[u]:2 * step * pair[u] + step + W],
                                     out[:, :], cs[u], sem, topo) for i, u in enumerate(group)], local_sem=T.sem.loc)
            n += len(order)
        return n

    def own_plane(waits, src, out, arr, buf, sem):
        n = 0
        for (kind, ks), w in zip(PLAN, waits):
            for s, m in w:
                g.wait_ge(s, m)
            if kind == "straight":
                g.remote_dma_fused([send(share(off, i, len(ks)), src(k), out, T.cores[others[k]], arr, topo)
                                    for i, k in enumerate(ks)], local_sem=T.sem.loc)
            else:
                g.remote_dma_fused([send(share(inner, i, len(ks)), src(k), buf[:, 0:W], cs[HELPER[k]], sem, topo)
                                    for i, k in enumerate(ks)], local_sem=T.sem.loc)
            n += 8
        return n

    def piece(k):
        b = place(others[k], pl)[1]
        return T.XS[:, W * b:W * b + W]
    nloc += to_ports([[(T.sem["ld%d" % i], 16 * len(gr))] for i, gr in enumerate(GROUPS)], T.XC, W, T.HA, T.sem.ha)
    nloc += own_plane([[(T.sem.lds, 16)], [], []], piece, T.W[:, rank * W:(rank + 1) * W], T.sem.arr1, T.HA, T.sem.ha)

    vec = g.vector
    n = [0]
    v = chain(vec, T.sem.vc, n)
    vec.wait_ge(T.sem.io1, 2)
    v(vec.tensor_scalar(T.SEL[0:16, :], T.HD[0:16, :], 0, None, eq),
      vec.tensor_scalar(T.K0[0:16, 0:1], T.P[0:16, 0:1], 16, None, mult),
      vec.tensor_scalar(T.KN[0:16, 0:1], T.P[0:16, 0:1], -16, None, mult),
      vec.tensor_scalar(T.KT[0:16, 0:1], T.P[0:16, 0:1], 16, NW, mult, add))
    vec.wait_ge(T.sem.ldh, 16)
    v(vec.tensor_scalar(T.QI[0:16, 0:1], T.HH[0:16, 0:1], 11, None, shr),
      vec.tensor_scalar(T.RI[0:16, 0:1], T.HH[0:16, 0:1], COLS - 1, None, band))
    v(vec.tensor_scalar(T.RH[0:16, 0:1], T.RI[0:16, 0:1], T.K0[0:16, 0:1], None, add),
      vec.tensor_scalar(T.RH[0:16, 1:2], T.QI[0:16, 0:1], -W, T.KT[0:16, 0:1], mult, add),
      vec.tensor_scalar(T.RH[0:16, 2:3], T.QI[0:16, 0:1], W, T.KN[0:16, 0:1], mult, add),
      vec.tensor_scalar(T.RH[0:16, 3:4], T.RI[0:16, 0:1], T.KN[0:16, 0:1], None, add))
    g.tensor.wait_ge(T.sem.vc, n[0])
    g.tensor.matmul(T.ps[:, 0:4], T.SEL[0:16, :], T.RH[0:16, 0:4], True, True).then_inc(T.sem.pe, 1)
    vec.wait_ge(T.sem.tab, 3 * len(off) + 8)
    vec.wait_ge(T.sem.pe, 1)
    v(vec.tensor_scalar(T.M[:, :], T.TA[:, :], T.ps[:, 0:1], W, lt, mult))
    v(vec.tensor_tensor(T.V[:, :], T.E[:, :], T.M[:, :], add))
    v(vec.tensor_scalar(T.O[:, :], T.V[:, :], T.ps[:, 1:2], -NW, ge, mult))
    v(vec.tensor_tensor(T.R[:, :], T.V[:, :], T.O[:, :], add))
    v(vec.tensor_scalar(T.L1[:, :], T.R[:, :], T.ps[:, 2:3], NW - 1, add, low),
      vec.tensor_copy(T.SM[:, 0:1], T.ps[:, 3:4]))
    g.wait_ge(T.sem.vc, n[0])
    nloc += to_list_core(T.SM[:, 0:1], T.sem.sm, inner)

    g.scalar.wait_ge(T.sem.vc, n[0])
    for q in (vec, g.scalar):
        q.wait_ge(T.sem.own1, 16)
        q.wait_ge(T.sem.arr1, landed)
    queue = [(2 * pair[u] + e, T.sem["ga%d" % u]) for u in range(3) for e in range(2)]
    queue += [(6 + k, T.sem["go%d" % i]) for i, (kind, ks) in enumerate(PLAN) for k in ks] + [(11, T.sem.gown)]
    for e, (i, sem) in enumerate(queue):
        out, src = T.OUT[:, i * G:(i + 1) * G], T.W[:, :].indirect(T.L1[:, i * KP:i * KP + K])
        ins = g.scalar.activation(out, src, copy) if e % 2 else vec.tensor_copy(out, src)
        ins.then_inc(sem, 1)
    g.sync.wait_ge(T.sem.gown, 1)
    g.sync.dma_start(T.Z[:, zs:zs + W], T.OUT[:, 11 * G:11 * G + W]).then_inc(T.sem.own2, 16)

    def gathered(k):
        return T.OUT[:, (6 + k) * G:(6 + k) * G + W]
    nloc += to_ports([[(T.sem["ga%d" % u], 2) for u in gr] for gr in GROUPS], T.OUT, G, T.HB, T.sem.hb)
    nloc += own_plane([[(T.sem["go%d" % i], len(ks))] for i, (kind, ks) in enumerate(PLAN)], gathered,
                      T.Z[:, zs:zs + W], T.sem.arr2, T.HB, T.sem.hb)

    for q in (vec, g.scalar):
        q.wait_ge(T.sem.l2, 8)
        q.wait_ge(T.sem.own2, 16)
        q.wait_ge(T.sem.arr2, landed)
    blocks = [512 * b + COLS // 2 * e for b in range(2) for e in range(2)]
    for b, c in enumerate(blocks):
        out, src = T.YO[:, c:c + 512], T.Z[:, :].indirect(T.L2[:, c // 16:c // 16 + 32])
        ins = g.scalar.activation(out, src, copy) if b % 2 else vec.tensor_copy(out, src)
        ins.then_inc(T.sem["y%d" % b], 1)
    for b, c in enumerate(blocks):
        q, st = (g.scalar, T.sem.st2) if b == 3 else (g.sync, T.sem.st)
        q.wait_ge(T.sem["y%d" % b], 1)
        q.dma_start(T.y[:, c:c + 512], T.YO[:, c:c + 512]).then_inc(st, 16)
    g.sync.wait_ge(T.sem.st, 48)
    g.scalar.wait_ge(T.sem.st2, 16)
    g.wait_ge(T.sem.loc, nloc)
